import numpy as np
import ml_dtypes


def mxq(x, axis, fmt="e4m3"):
    dtype, down = {"e4m3": (ml_dtypes.float8_e4m3fn, 7), "e5m2": (ml_dtypes.float8_e5m2, 14)}[fmt]
    v = np.moveaxis(np.asarray(x, np.float32).astype(ml_dtypes.bfloat16).astype(np.float64), axis, -1)
    blocks = v.reshape(v.shape[:-1] + (-1, 32))
    amax = np.abs(blocks).max(-1, keepdims=True)
    byte = np.maximum(np.where(amax > 0, np.frexp(amax)[1] - 1 + 127, 0) - down, 1)
    scale = np.exp2(byte - 127.0)
    codes = (blocks / scale).astype(np.float32).astype(dtype).astype(np.float64)
    return np.moveaxis((codes * scale).reshape(v.shape), -1, axis)


WIDE = False


def mx_kscale(k, group=512):
    if not WIDE:
        return np.ones(k)
    levels = np.array([18, -18])
    if group != 512:
        return np.exp2(np.random.permutation(np.resize(levels, k // group))).repeat(group)
    if k % 512:
        return np.exp2(np.random.permutation(np.resize(levels, k // 32))).repeat(32)
    a = np.empty((k // 512, 16))
    for p in range(k // 512):
        a[p, :8] = np.random.permutation(np.resize(levels, 8))
        for g in range(8):
            far = levels[np.abs(levels - a[p, g]) >= 10]
            a[p, g + 8] = far[np.random.randint(len(far))]
    return np.exp2(a.ravel()).repeat(32)


def f64(x):
    return np.asarray(x).astype(np.float64)


G, D, M, O, N = 4, 128, 128, 128, 512


def sgn(shape):
    return np.random.uniform(0.5, 2.0, shape) * np.where(np.random.standard_normal(shape) < 0, -1.0, 1.0)


def setup_inputs():
    n = np.random.standard_normal
    s_d = mx_kscale(D, 0)
    s_m = mx_kscale(M, 0)
    return {
        "x": (n((G, D, N)) * s_d[:, None]).astype(np.float32),
        "w1": (n((G, D, M)) / np.sqrt(D) / s_d[:, None]).astype(np.float32),
        "w2": (n((G, D, M)) / np.sqrt(D) / s_d[:, None]).astype(np.float32),
        "ra": (np.random.uniform(0.3, 1.5, (G, M, 1))).astype(np.float32),
        "hs": (sgn((G, M, 1)) * s_m[:, None]).astype(np.float32),
        "wo2": (n((G, M, O)) / np.sqrt(M) / s_m[:, None]).astype(np.float32),
        "res": (0.5 * n((G, O, N))).astype(np.float32),
    }


def reference(x, w1, w2, ra, hs, wo2, res):
    w1q = mxq(f64(w1), 1, "e4m3")
    xq = mxq(f64(x), 1, "e4m3")
    z1 = w1q.transpose(0, 2, 1) @ xq
    w2q = mxq(f64(w2), 1, "e4m3")
    z2 = w2q.transpose(0, 2, 1) @ xq
    nn = np.sqrt(np.square(z1) + np.square(z2) + f64(ra))
    h = z1 / nn
    hh = h * f64(hs)
    wo2q = mxq(f64(wo2), 1, "e4m3")
    hhq = mxq(hh, 1, "e4m3")
    y0 = wo2q.transpose(0, 2, 1) @ hhq
    y = y0 + f64(res)
    return y

@@ -1,0 +1,171 @@
+from contextlib import ExitStack
+
+import concourse.mybir as mybir
+
+G, D, M, O, N = 4, 128, 128, 128, 512
+FLOPS = 2 * G * N * (2 * D * M + M * O)
+
+F32 = mybir.dt.float32
+BF16 = mybir.dt.bfloat16
+U32 = mybir.dt.uint32
+U8 = mybir.dt.uint8
+FP8X4 = mybir.dt.float8_e4m3fn_x4
+ACT = mybir.ActivationFunctionType
+ALU = mybir.AluOpType
+
+P = 128
+PACK = 4
+R = 32
+NT = 128
+HALF = 256
+CHUNKS = ((0, 256), (256, 128), (384, 128))
+LAG = 2
+
+
+def interleave(copy, dst, src):
+    copy(out=dst.rearrange("p (c i) t -> p c t i", i=4), in_=src.rearrange("p t (c i) -> p c t i", i=4))
+
+
+def tile_rows_fsphere_kernel(tc, x, w1, w2, ra, hs, wo2, res, out):
+    nc = tc.nc
+    with ExitStack() as ctx:
+        sb = ctx.enter_context(tc.tile_pool(name="sb", bufs=1))
+        ps = ctx.enter_context(tc.psum_pool(name="ps", bufs=1))
+        ctx.enter_context(tc.manual_schedule())
+
+        def packed(name, width):
+            grouped = sb.tile([P, width, PACK], BF16, name=name + "_bf", align_bytes=64)
+            codes = sb.tile([P, width], U32, name=name + "_codes", align_bytes=64)
+            scales = sb.tile([P, width], U8, name=name + "_scales", align_bytes=64)
+            return grouped, codes, scales
+
+        def quantize(op):
+            nc.vector.quantize_mx(out=op[1][:].bitcast(FP8X4), scales=op[2][:],
+                                  in_=op[0][:].rearrange("p w j -> p (w j)"))
+
+        def mm(dst, g, wq, xq, col):
+            rows = slice(R * g, R * g + R)
+            nc.tensor.matmul_mx(out=dst, lhsT=wq[1][rows, :].bitcast(FP8X4), lhsT_scale=wq[2][rows, :],
+                                rhs=xq[1][rows, col:col + NT].bitcast(FP8X4), rhs_scale=xq[2][rows, col:col + NT],
+                                start=True, stop=True)
+
+        banks = [[ps.tile([P, 512], F32, name="bank%d_%d" % (g, h)) for h in range(2)] for g in range(G)]
+
+        x_rows = x.rearrange("g (p j) n -> (g p) j n", j=PACK)
+        x_raw = [sb.tile([P, PACK, HALF], F32, name="x_raw%d" % h) for h in range(2)]
+        w_raw = [sb.tile([P, PACK, M], F32, name="w_raw%d" % i) for i in range(3)]
+        res_sb = sb.tile([P, G, N], F32, name="res_sb")
+        vec_rows = sb.tile([P, P], F32, name="vec_rows", align_bytes=64)
+        vec = sb.tile([P, P], F32, name="vec", align_bytes=64)
+
+        nc.gpsimd.memset(vec_rows[:], 0.0)
+        nc.sync.dma_start(out=x_raw[0][:], in_=x_rows[:, :, 0:HALF])
+        for i, w in enumerate((w1, w2, wo2)):
+            nc.sync.dma_start(out=w_raw[i][:], in_=w.rearrange("g (p j) m -> (g p) j m", j=PACK))
+        nc.sync.dma_start(out=x_raw[1][:], in_=x_rows[:, :, HALF:N])
+        nc.sync.dma_start(out=res_sb[:], in_=res.rearrange("g o n -> o g n"))
+        for i, v in enumerate((ra, hs)):
+            nc.scalar.dma_start(out=vec_rows[i:P:R, :].rearrange("b (g j) -> b g j", g=G),
+                                in_=v.rearrange("g (b j) one -> b g (j one)", j=R))
+
+        xq = [packed("xq%d" % h, HALF) for h in range(2)]
+        wq = [packed("wq%d" % i, M) for i in range(3)]
+
+        interleave(nc.vector.tensor_copy, xq[0][0][:], x_raw[0][:])
+        interleave(nc.scalar.copy, wq[0][0][:], w_raw[0][:])
+        nc.vector.transpose(vec[:], vec_rows[:])
+        quantize(xq[0])
+        interleave(nc.vector.tensor_copy, wq[1][0][:], w_raw[1][:])
+        quantize(wq[0])
+        quantize(wq[1])
+        interleave(nc.scalar.copy, wq[2][0][:], w_raw[2][:])
+
+        def first_layer(h):
+            for g in range(G):
+                for i in range(2):
+                    for col in range(0, HALF, NT):
+                        mm(banks[g][h][:, i * HALF + col:i * HALF + col + NT], g, wq[i], xq[h], col)
+
+        first_layer(0)
+
+        units = [(k, g) for k in range(len(CHUNKS)) for g in range(G)]
+        sq, tot, rin, hh = {}, {}, {}, {}
+        stage = [sb.tile([P, PACK, w], BF16, name="stage%d" % k) for k, (c, w) in enumerate(CHUNKS)]
+        hq = [packed("hq%d" % k, w) for k, (c, w) in enumerate(CHUNKS)]
+        out_sb = [sb.tile([P, G, w], F32, name="out_sb%d" % k) for k, (c, w) in enumerate(CHUNKS)]
+        out_rows = out.rearrange("g o n -> o g n")
+
+        def zview(u):
+            k, g = units[u]
+            c, w = CHUNKS[k]
+            return banks[g][c // HALF][:].rearrange("p (t n) -> p t n", t=2)[:, :, c % HALF:c % HALF + w]
+
+        def squares(u):
+            w = CHUNKS[units[u][0]][1]
+            sq[u] = sb.tile([P, 2, w], F32, name="sq%d" % u)
+            nc.scalar.activation(out=sq[u][:], in_=zview(u), func=ACT.Square)
+
+        def add(u):
+            w = CHUNKS[units[u][0]][1]
+            tot[u] = sb.tile([P, w], F32, name="tot%d" % u)
+            nc.vector.tensor_tensor(out=tot[u][:], in0=sq[u][:, 0, :], in1=sq[u][:, 1, :], op=ALU.add)
+
+        def root(u):
+            k, g = units[u]
+            w = CHUNKS[k][1]
+            rin[u] = sb.tile([P, w], F32, name="rin%d" % u)
+            nc.scalar.activation(out=rin[u][:], in_=tot[u][:], func=ACT.Abs_reciprocal_sqrt,
+                                 bias=vec[:, R * g:R * g + 1])
+
+        def scale_and_move(u):
+            k, g = units[u]
+            w = CHUNKS[k][1]
+            hh[u] = sb.tile([P, w], BF16, name="hh%d" % u)
+            nc.vector.scalar_tensor_tensor(out=hh[u][:], in0=zview(u)[:, 0, :], scalar=vec[:, R * g + 1:R * g + 2],
+                                           in1=rin[u][:], op0=ALU.mult, op1=ALU.mult)
+            nc.sync.dma_start(out=stage[k][R * g:R * g + R, :, :], in_=hh[u][:])
+
+        def second_layer(k):
+            c, w = CHUNKS[k]
+            for g in range(G):
+                for col in range(0, w, NT):
+                    mm(banks[g][0][:, c + col:c + col + NT], g, wq[2], hq[k], col)
+
+        def finish(k):
+            c, w = CHUNKS[k]
+            for g in range(G):
+                nc.vector.tensor_tensor(out=out_sb[k][:, g, :], in0=banks[g][0][:, c:c + w],
+                                        in1=res_sb[:, g, c:c + w], op=ALU.add)
+            nc.sync.dma_start(out=out_rows[:, :, c:c + w], in_=out_sb[k][:])
+
+        for s in range(len(units) + LAG):
+            if s < len(units):
+                squares(s)
+            if s >= LAG:
+                root(s - LAG)
+            if s < len(units):
+                add(s)
+            if s >= LAG:
+                scale_and_move(s - LAG)
+            if s == 0:
+                interleave(nc.vector.tensor_copy, xq[1][0][:], x_raw[1][:])
+            if s == 1:
+                quantize(xq[1])
+                first_layer(1)
+            if s == 2:
+                quantize(wq[2])
+            if s == 9:
+                interleave(nc.vector.tensor_copy, hq[0][0][:], stage[0][:])
+            if s == 10:
+                quantize(hq[0])
+                second_layer(0)
+
+        interleave(nc.scalar.copy, hq[1][0][:], stage[1][:])
+        finish(0)
+        quantize(hq[1])
+        second_layer(1)
+        interleave(nc.vector.tensor_copy, hq[2][0][:], stage[2][:])
+        finish(1)
+        quantize(hq[2])
+        second_layer(2)
+        finish(2)

@@ -10,20 +10,27 @@ BF16 = mybir.dt.bfloat16
 U32 = mybir.dt.uint32
 U8 = mybir.dt.uint8
 FP8X4 = mybir.dt.float8_e4m3fn_x4
-ACT = mybir.ActivationFunctionType
+FUNC = mybir.ActivationFunctionType
 ALU = mybir.AluOpType
 
 P = 128
 PACK = 4
-R = 32
-NT = 128
-HALF = 256
-CHUNKS = ((0, 256), (256, 128), (384, 128))
+ROWS = 32
+W = 128
+CHUNKS = N // W
+UNITS = CHUNKS * G
+BANK = 512
+
+X_LOADS = ((0, 1), (1, 1), (2, 2))
 LAG = 2
+X_EVERY = 3
+WO_STEP = X_EVERY * (CHUNKS - 2) + 1
+HH_STEP = 12
+SCALAR_COLS = 48
 
 
 def interleave(copy, dst, src):
-    copy(out=dst.rearrange("p (c i) t -> p c t i", i=4), in_=src.rearrange("p t (c i) -> p c t i", i=4))
+    copy(out=dst.rearrange("p (c i) j -> p c j i", i=4), in_=src.rearrange("p j (c i) -> p c j i", i=4))
 
 
 def tile_rows_fsphere_kernel(tc, x, w1, w2, ra, hs, wo2, res, out):
@@ -33,139 +40,162 @@ def tile_rows_fsphere_kernel(tc, x, w1, w2, ra, hs, wo2, res, out):
         ps = ctx.enter_context(tc.psum_pool(name="ps", bufs=1))
         ctx.enter_context(tc.manual_schedule())
 
-        def packed(name, width):
-            grouped = sb.tile([P, width, PACK], BF16, name=name + "_bf", align_bytes=64)
-            codes = sb.tile([P, width], U32, name=name + "_codes", align_bytes=64)
-            scales = sb.tile([P, width], U8, name=name + "_scales", align_bytes=64)
+        def operand(name):
+            grouped = sb.tile([P, W, PACK], BF16, name=name + "_bf", align_bytes=64)
+            codes = sb.tile([P, W], U32, name=name + "_codes", align_bytes=64)
+            scales = sb.tile([P, W], U8, name=name + "_scales", align_bytes=64)
             return grouped, codes, scales
 
-        def quantize(op):
-            nc.vector.quantize_mx(out=op[1][:].bitcast(FP8X4), scales=op[2][:],
-                                  in_=op[0][:].rearrange("p w j -> p (w j)"))
+        def interleave_shared(op, src):
+            interleave(nc.scalar.copy, op[0][:, 0:SCALAR_COLS, :], src[:, :, 0:SCALAR_COLS])
+            interleave(nc.vector.tensor_copy, op[0][:, SCALAR_COLS:W, :], src[:, :, SCALAR_COLS:W])
 
-        def mm(dst, g, wq, xq, col):
-            rows = slice(R * g, R * g + R)
-            nc.tensor.matmul_mx(out=dst, lhsT=wq[1][rows, :].bitcast(FP8X4), lhsT_scale=wq[2][rows, :],
-                                rhs=xq[1][rows, col:col + NT].bitcast(FP8X4), rhs_scale=xq[2][rows, col:col + NT],
+        def quantize(op):
+            grouped, codes, scales = op
+            nc.vector.quantize_mx(out=codes[:].bitcast(FP8X4), scales=scales[:],
+                                  in_=grouped[:].rearrange("p w j -> p (w j)"))
+
+        def product(dst, g, weights, moving):
+            rows = slice(ROWS * g, ROWS * (g + 1))
+            nc.tensor.matmul_mx(out=dst, lhsT=weights[1][rows, :].bitcast(FP8X4), lhsT_scale=weights[2][rows, :],
+                                rhs=moving[1][rows, :].bitcast(FP8X4), rhs_scale=moving[2][rows, :],
                                 start=True, stop=True)
 
-        banks = [[ps.tile([P, 512], F32, name="bank%d_%d" % (g, h)) for h in range(2)] for g in range(G)]
+        banks = [[ps.tile([P, BANK], F32, name="bank%d_%d" % (g, b)) for b in range(2)] for g in range(G)]
 
-        x_rows = x.rearrange("g (p j) n -> (g p) j n", j=PACK)
-        x_raw = [sb.tile([P, PACK, HALF], F32, name="x_raw%d" % h) for h in range(2)]
+        x_raw = [sb.tile([P, PACK, n * W], F32, name="x_raw%d" % k) for k, n in X_LOADS]
         w_raw = [sb.tile([P, PACK, M], F32, name="w_raw%d" % i) for i in range(3)]
         res_sb = sb.tile([P, G, N], F32, name="res_sb")
         vec_rows = sb.tile([P, P], F32, name="vec_rows", align_bytes=64)
         vec = sb.tile([P, P], F32, name="vec", align_bytes=64)
+        warm = sb.tile([P, 2], F32, name="warm")
 
-        nc.gpsimd.memset(vec_rows[:], 0.0)
-        nc.sync.dma_start(out=x_raw[0][:], in_=x_rows[:, :, 0:HALF])
+        x_rows = x.rearrange("g (p j) n -> (g p) j n", j=PACK)
+
+        def load_x(i):
+            k, n = X_LOADS[i]
+            nc.sync.dma_start(out=x_raw[i][:], in_=x_rows[:, :, k * W:(k + n) * W])
+
+        def x_chunk(k):
+            i = max(i for i, (first, n) in enumerate(X_LOADS) if first <= k)
+            col = (k - X_LOADS[i][0]) * W
+            return x_raw[i][:, :, col:col + W]
+
+        nc.vector.memset(vec_rows[:], 0.0)
+        nc.vector.memset(warm[:, 0:1], 1.0)
+        load_x(0)
+        for i, v in enumerate((ra, hs)):
+            nc.sync.dma_start(out=vec_rows[i:P:ROWS, :].rearrange("b (g j) -> b g j", g=G),
+                              in_=v.rearrange("g (b j) one -> b g (j one)", j=ROWS))
         for i, w in enumerate((w1, w2, wo2)):
             nc.sync.dma_start(out=w_raw[i][:], in_=w.rearrange("g (p j) m -> (g p) j m", j=PACK))
-        nc.sync.dma_start(out=x_raw[1][:], in_=x_rows[:, :, HALF:N])
+        for i in range(1, len(X_LOADS)):
+            load_x(i)
         nc.sync.dma_start(out=res_sb[:], in_=res.rearrange("g o n -> o g n"))
-        for i, v in enumerate((ra, hs)):
-            nc.scalar.dma_start(out=vec_rows[i:P:R, :].rearrange("b (g j) -> b g j", g=G),
-                                in_=v.rearrange("g (b j) one -> b g (j one)", j=R))
 
-        xq = [packed("xq%d" % h, HALF) for h in range(2)]
-        wq = [packed("wq%d" % i, M) for i in range(3)]
+        nc.scalar.activation(out=warm[:, 1:2], in_=warm[:, 0:1], func=FUNC.Abs_reciprocal_sqrt)
 
-        interleave(nc.vector.tensor_copy, xq[0][0][:], x_raw[0][:])
-        interleave(nc.scalar.copy, wq[0][0][:], w_raw[0][:])
-        nc.vector.transpose(vec[:], vec_rows[:])
-        quantize(xq[0])
-        interleave(nc.vector.tensor_copy, wq[1][0][:], w_raw[1][:])
-        quantize(wq[0])
-        quantize(wq[1])
-        interleave(nc.scalar.copy, wq[2][0][:], w_raw[2][:])
-
-        def first_layer(h):
-            for g in range(G):
-                for i in range(2):
-                    for col in range(0, HALF, NT):
-                        mm(banks[g][h][:, i * HALF + col:i * HALF + col + NT], g, wq[i], xq[h], col)
-
-        first_layer(0)
-
-        units = [(k, g) for k in range(len(CHUNKS)) for g in range(G)]
-        sq, tot, rin, hh = {}, {}, {}, {}
-        stage = [sb.tile([P, PACK, w], BF16, name="stage%d" % k) for k, (c, w) in enumerate(CHUNKS)]
-        hq = [packed("hq%d" % k, w) for k, (c, w) in enumerate(CHUNKS)]
-        out_sb = [sb.tile([P, G, w], F32, name="out_sb%d" % k) for k, (c, w) in enumerate(CHUNKS)]
+        xq = [operand("xq%d" % k) for k in range(CHUNKS)]
+        w1q, w2q, wo2q = (operand("wq%d" % i) for i in range(3))
+        hq = [operand("hq%d" % k) for k in range(CHUNKS)]
+        hh_rows = [sb.tile([P, PACK, W], BF16, name="hh_rows%d" % k) for k in range(CHUNKS)]
+        out_sb = [sb.tile([P, G, W], F32, name="out_sb%d" % k) for k in range(CHUNKS)]
         out_rows = out.rearrange("g o n -> o g n")
+        squares = [sb.tile([P, 2 * W], F32, name="squares%d" % u) for u in range(UNITS)]
+        total = [sb.tile([P, W], F32, name="total%d" % u) for u in range(UNITS)]
+        inv_norm = [sb.tile([P, W], F32, name="inv_norm%d" % u) for u in range(UNITS)]
+        hh = [sb.tile([P, W], BF16, name="hh%d" % u) for u in range(UNITS)]
 
-        def zview(u):
-            k, g = units[u]
-            c, w = CHUNKS[k]
-            return banks[g][c // HALF][:].rearrange("p (t n) -> p t n", t=2)[:, :, c % HALF:c % HALF + w]
+        def first_layer(k):
+            for g in range(G):
+                product(banks[g][k % 2][:, 0:W], g, w1q, xq[k])
+                product(banks[g][k % 2][:, W:2 * W], g, w2q, xq[k])
 
-        def squares(u):
-            w = CHUNKS[units[u][0]][1]
-            sq[u] = sb.tile([P, 2, w], F32, name="sq%d" % u)
-            nc.scalar.activation(out=sq[u][:], in_=zview(u), func=ACT.Square)
+        def square(u):
+            k, g = divmod(u, G)
+            nc.scalar.activation(out=squares[u][:], in_=banks[g][k % 2][:, 0:2 * W], func=FUNC.Square)
 
         def add(u):
-            w = CHUNKS[units[u][0]][1]
-            tot[u] = sb.tile([P, w], F32, name="tot%d" % u)
-            nc.vector.tensor_tensor(out=tot[u][:], in0=sq[u][:, 0, :], in1=sq[u][:, 1, :], op=ALU.add)
+            nc.vector.tensor_tensor(out=total[u][:], in0=squares[u][:, 0:W], in1=squares[u][:, W:2 * W], op=ALU.add)
 
-        def root(u):
-            k, g = units[u]
-            w = CHUNKS[k][1]
-            rin[u] = sb.tile([P, w], F32, name="rin%d" % u)
-            nc.scalar.activation(out=rin[u][:], in_=tot[u][:], func=ACT.Abs_reciprocal_sqrt,
-                                 bias=vec[:, R * g:R * g + 1])
+        def inverse_root(u):
+            g = u % G
+            nc.scalar.activation(out=inv_norm[u][:], in_=total[u][:], func=FUNC.Abs_reciprocal_sqrt,
+                                 bias=vec[:, ROWS * g:ROWS * g + 1])
 
         def scale_and_move(u):
-            k, g = units[u]
-            w = CHUNKS[k][1]
-            hh[u] = sb.tile([P, w], BF16, name="hh%d" % u)
-            nc.vector.scalar_tensor_tensor(out=hh[u][:], in0=zview(u)[:, 0, :], scalar=vec[:, R * g + 1:R * g + 2],
-                                           in1=rin[u][:], op0=ALU.mult, op1=ALU.mult)
-            nc.sync.dma_start(out=stage[k][R * g:R * g + R, :, :], in_=hh[u][:])
+            k, g = divmod(u, G)
+            nc.vector.scalar_tensor_tensor(out=hh[u][:], in0=banks[g][k % 2][:, 0:W],
+                                           scalar=vec[:, ROWS * g + 1:ROWS * g + 2], in1=inv_norm[u][:],
+                                           op0=ALU.mult, op1=ALU.mult)
+            nc.sync.dma_start(out=hh_rows[k][ROWS * g:ROWS * (g + 1), :, :], in_=hh[u][:])
 
         def second_layer(k):
-            c, w = CHUNKS[k]
             for g in range(G):
-                for col in range(0, w, NT):
-                    mm(banks[g][0][:, c + col:c + col + NT], g, wq[2], hq[k], col)
+                product(banks[g][k % 2][:, 2 * W:3 * W], g, wo2q, hq[k])
 
-        def finish(k):
-            c, w = CHUNKS[k]
-            for g in range(G):
-                nc.vector.tensor_tensor(out=out_sb[k][:, g, :], in0=banks[g][0][:, c:c + w],
-                                        in1=res_sb[:, g, c:c + w], op=ALU.add)
-            nc.sync.dma_start(out=out_rows[:, :, c:c + w], in_=out_sb[k][:])
+        def add_residual(k, groups):
+            for g in groups:
+                nc.vector.tensor_tensor(out=out_sb[k][:, g, :], in0=banks[g][k % 2][:, 2 * W:3 * W],
+                                        in1=res_sb[:, g, k * W:(k + 1) * W], op=ALU.add)
 
-        for s in range(len(units) + LAG):
-            if s < len(units):
-                squares(s)
-            if s >= LAG:
-                root(s - LAG)
-            if s < len(units):
-                add(s)
-            if s >= LAG:
-                scale_and_move(s - LAG)
-            if s == 0:
-                interleave(nc.vector.tensor_copy, xq[1][0][:], x_raw[1][:])
-            if s == 1:
-                quantize(xq[1])
-                first_layer(1)
-            if s == 2:
-                quantize(wq[2])
-            if s == 9:
-                interleave(nc.vector.tensor_copy, hq[0][0][:], stage[0][:])
-            if s == 10:
+        def store(queue, k, g0, g1):
+            queue.dma_start(out=out_rows[:, g0:g1, k * W:(k + 1) * W], in_=out_sb[k][:, g0:g1, :])
+
+        interleave(nc.vector.tensor_copy, xq[0][0][:], x_chunk(0))
+        nc.vector.transpose(vec[:], vec_rows[:])
+        quantize(xq[0])
+        interleave(nc.vector.tensor_copy, w1q[0][:], w_raw[0][:])
+        interleave_shared(w2q, w_raw[1])
+        quantize(w1q)
+        quantize(w2q)
+        first_layer(0)
+        interleave(nc.scalar.copy, wo2q[0][:], w_raw[2][:])
+        interleave(nc.vector.tensor_copy, xq[1][0][:], x_chunk(1))
+
+        for step in range(UNITS + LAG):
+            if step < UNITS:
+                square(step)
+            if step >= LAG:
+                inverse_root(step - LAG)
+            if step < UNITS:
+                add(step)
+            if step >= LAG:
+                scale_and_move(step - LAG)
+
+            for k in range(1, CHUNKS):
+                quantize_step = X_EVERY * (k - 1)
+                banks_free_step = G * (k - 1) - 1 + LAG if k >= 2 else 0
+                if step == quantize_step:
+                    quantize(xq[k])
+                if step == max(quantize_step, banks_free_step):
+                    first_layer(k)
+                if step == quantize_step - 1:
+                    interleave(nc.vector.tensor_copy, xq[k][0][:], x_chunk(k))
+            if step == WO_STEP:
+                quantize(wo2q)
+            if step == HH_STEP:
+                interleave(nc.vector.tensor_copy, hq[0][0][:], hh_rows[0][:])
+            if step == HH_STEP + 1:
                 quantize(hq[0])
                 second_layer(0)
 
-        interleave(nc.scalar.copy, hq[1][0][:], stage[1][:])
-        finish(0)
+        half = G // 2
+        interleave(nc.scalar.copy, hq[1][0][:], hh_rows[1][:])
+        add_residual(0, range(G))
+        store(nc.sync, 0, 0, G)
         quantize(hq[1])
         second_layer(1)
-        interleave(nc.vector.tensor_copy, hq[2][0][:], stage[2][:])
-        finish(1)
-        quantize(hq[2])
-        second_layer(2)
-        finish(2)
+        for k in range(2, CHUNKS):
+            interleave_shared(hq[k], hh_rows[k])
+            add_residual(k - 1, range(1))
+            quantize(hq[k])
+            second_layer(k)
+            if k < CHUNKS - 1:
+                add_residual(k - 1, range(1, G))
+                store(nc.sync, k - 1, 0, G)
+        for k, first in ((CHUNKS - 2, 1), (CHUNKS - 1, 0)):
+            add_residual(k, range(first, half))
+            store(nc.sync, k, 0, half)
+            add_residual(k, range(half, G))
+            store(nc.scalar, k, half, G)

@@ -23,10 +23,10 @@ BANK = 512
 
 X_LOADS = ((0, 1), (1, 1), (2, 2))
 LAG = 2
-X_EVERY = 3
-WO_STEP = X_EVERY * (CHUNKS - 2) + 1
-HH_STEP = 12
+WO_STEP = 2
+HH_STEP = 11
 SCALAR_COLS = 48
+RESIDUALS_FIRST = (2, 1, 2)
 
 
 def interleave(copy, dst, src):
@@ -45,10 +45,6 @@ def tile_rows_fsphere_kernel(tc, x, w1, w2, ra, hs, wo2, res, out):
             codes = sb.tile([P, W], U32, name=name + "_codes", align_bytes=64)
             scales = sb.tile([P, W], U8, name=name + "_scales", align_bytes=64)
             return grouped, codes, scales
-
-        def interleave_shared(op, src):
-            interleave(nc.scalar.copy, op[0][:, 0:SCALAR_COLS, :], src[:, :, 0:SCALAR_COLS])
-            interleave(nc.vector.tensor_copy, op[0][:, SCALAR_COLS:W, :], src[:, :, SCALAR_COLS:W])
 
         def quantize(op):
             grouped, codes, scales = op
@@ -146,12 +142,16 @@ def tile_rows_fsphere_kernel(tc, x, w1, w2, ra, hs, wo2, res, out):
         nc.vector.transpose(vec[:], vec_rows[:])
         quantize(xq[0])
         interleave(nc.vector.tensor_copy, w1q[0][:], w_raw[0][:])
-        interleave_shared(w2q, w_raw[1])
+        interleave(nc.scalar.copy, w2q[0][:, 0:SCALAR_COLS, :], w_raw[1][:, :, 0:SCALAR_COLS])
+        interleave(nc.vector.tensor_copy, w2q[0][:, SCALAR_COLS:M, :], w_raw[1][:, :, SCALAR_COLS:M])
         quantize(w1q)
         quantize(w2q)
         first_layer(0)
         interleave(nc.scalar.copy, wo2q[0][:], w_raw[2][:])
         interleave(nc.vector.tensor_copy, xq[1][0][:], x_chunk(1))
+
+        def last_read_step(k):
+            return G * (k + 1) - 1 + LAG
 
         for step in range(UNITS + LAG):
             if step < UNITS:
@@ -164,38 +164,38 @@ def tile_rows_fsphere_kernel(tc, x, w1, w2, ra, hs, wo2, res, out):
                 scale_and_move(step - LAG)
 
             for k in range(1, CHUNKS):
-                quantize_step = X_EVERY * (k - 1)
-                banks_free_step = G * (k - 1) - 1 + LAG if k >= 2 else 0
-                if step == quantize_step:
-                    quantize(xq[k])
-                if step == max(quantize_step, banks_free_step):
-                    first_layer(k)
+                quantize_step = G * (k - 1)
                 if step == quantize_step - 1:
                     interleave(nc.vector.tensor_copy, xq[k][0][:], x_chunk(k))
+                if step == quantize_step:
+                    quantize(xq[k])
+                banks_free_step = last_read_step(k - 2) if k >= 2 else 0
+                if step == max(quantize_step, banks_free_step):
+                    first_layer(k)
             if step == WO_STEP:
                 quantize(wo2q)
             if step == HH_STEP:
                 interleave(nc.vector.tensor_copy, hq[0][0][:], hh_rows[0][:])
             if step == HH_STEP + 1:
                 quantize(hq[0])
+            if step == last_read_step(2):
                 second_layer(0)
 
         half = G // 2
-        interleave(nc.scalar.copy, hq[1][0][:], hh_rows[1][:])
-        add_residual(0, range(G))
-        store(nc.sync, 0, 0, G)
-        quantize(hq[1])
-        second_layer(1)
-        for k in range(2, CHUNKS):
-            interleave_shared(hq[k], hh_rows[k])
-            add_residual(k - 1, range(1))
+        for k in range(1, CHUNKS):
+            done, first = k - 1, RESIDUALS_FIRST[k - 1]
+            in_halves = done == CHUNKS - 2
+            interleave(nc.scalar.copy, hq[k][0][:], hh_rows[k][:])
+            add_residual(done, range(first))
+            if in_halves:
+                store(nc.sync, done, 0, half)
             quantize(hq[k])
             second_layer(k)
-            if k < CHUNKS - 1:
-                add_residual(k - 1, range(1, G))
-                store(nc.sync, k - 1, 0, G)
-        for k, first in ((CHUNKS - 2, 1), (CHUNKS - 1, 0)):
-            add_residual(k, range(first, half))
-            store(nc.sync, k, 0, half)
-            add_residual(k, range(half, G))
-            store(nc.scalar, k, half, G)
+            add_residual(done, range(first, G))
+            if in_halves:
+                store(nc.scalar, done, half, G)
+            else:
+                store(nc.sync, done, 0, G)
+        for queue, g0 in ((nc.sync, 0), (nc.scalar, half)):
+            add_residual(CHUNKS - 1, range(g0, g0 + half))
+            store(queue, CHUNKS - 1, g0, g0 + half)

from contextlib import ExitStack

import concourse.mybir as mybir

G, D, M, O, N = 4, 128, 128, 128, 512
FLOPS = 2 * G * N * (2 * D * M + M * O)

F32 = mybir.dt.float32
BF16 = mybir.dt.bfloat16
U32 = mybir.dt.uint32
U8 = mybir.dt.uint8
FP8X4 = mybir.dt.float8_e4m3fn_x4
FUNC = mybir.ActivationFunctionType
ALU = mybir.AluOpType

P = 128
PACK = 4
ROWS = 32
W = 128
CHUNKS = N // W
UNITS = CHUNKS * G
BANK = 512

X_LOADS = ((0, 1), (1, 1), (2, 2))
LAG = 2
WO_STEP = 2
HH_STEP = 11
SCALAR_COLS = 48
RESIDUALS_FIRST = (2, 1, 2)


def interleave(copy, dst, src):
    copy(out=dst.rearrange("p (c i) j -> p c j i", i=4), in_=src.rearrange("p j (c i) -> p c j i", i=4))


def tile_rows_fsphere_kernel(tc, x, w1, w2, ra, hs, wo2, res, out):
    nc = tc.nc
    with ExitStack() as ctx:
        sb = ctx.enter_context(tc.tile_pool(name="sb", bufs=1))
        ps = ctx.enter_context(tc.psum_pool(name="ps", bufs=1))
        ctx.enter_context(tc.manual_schedule())

        def operand(name):
            grouped = sb.tile([P, W, PACK], BF16, name=name + "_bf", align_bytes=64)
            codes = sb.tile([P, W], U32, name=name + "_codes", align_bytes=64)
            scales = sb.tile([P, W], U8, name=name + "_scales", align_bytes=64)
            return grouped, codes, scales

        def quantize(op):
            grouped, codes, scales = op
            nc.vector.quantize_mx(out=codes[:].bitcast(FP8X4), scales=scales[:],
                                  in_=grouped[:].rearrange("p w j -> p (w j)"))

        def product(dst, g, weights, moving):
            rows = slice(ROWS * g, ROWS * (g + 1))
            nc.tensor.matmul_mx(out=dst, lhsT=weights[1][rows, :].bitcast(FP8X4), lhsT_scale=weights[2][rows, :],
                                rhs=moving[1][rows, :].bitcast(FP8X4), rhs_scale=moving[2][rows, :],
                                start=True, stop=True)

        banks = [[ps.tile([P, BANK], F32, name="bank%d_%d" % (g, b)) for b in range(2)] for g in range(G)]

        x_raw = [sb.tile([P, PACK, n * W], F32, name="x_raw%d" % k) for k, n in X_LOADS]
        w_raw = [sb.tile([P, PACK, M], F32, name="w_raw%d" % i) for i in range(3)]
        res_sb = sb.tile([P, G, N], F32, name="res_sb")
        vec_rows = sb.tile([P, P], F32, name="vec_rows", align_bytes=64)
        vec = sb.tile([P, P], F32, name="vec", align_bytes=64)
        warm = sb.tile([P, 2], F32, name="warm")

        x_rows = x.rearrange("g (p j) n -> (g p) j n", j=PACK)

        def load_x(i):
            k, n = X_LOADS[i]
            nc.sync.dma_start(out=x_raw[i][:], in_=x_rows[:, :, k * W:(k + n) * W])

        def x_chunk(k):
            i = max(i for i, (first, n) in enumerate(X_LOADS) if first <= k)
            col = (k - X_LOADS[i][0]) * W
            return x_raw[i][:, :, col:col + W]

        nc.vector.memset(vec_rows[:], 0.0)
        nc.vector.memset(warm[:, 0:1], 1.0)
        load_x(0)
        for i, v in enumerate((ra, hs)):
            nc.sync.dma_start(out=vec_rows[i:P:ROWS, :].rearrange("b (g j) -> b g j", g=G),
                              in_=v.rearrange("g (b j) one -> b g (j one)", j=ROWS))
        for i, w in enumerate((w1, w2, wo2)):
            nc.sync.dma_start(out=w_raw[i][:], in_=w.rearrange("g (p j) m -> (g p) j m", j=PACK))
        for i in range(1, len(X_LOADS)):
            load_x(i)
        nc.sync.dma_start(out=res_sb[:], in_=res.rearrange("g o n -> o g n"))

        nc.scalar.activation(out=warm[:, 1:2], in_=warm[:, 0:1], func=FUNC.Abs_reciprocal_sqrt)

        xq = [operand("xq%d" % k) for k in range(CHUNKS)]
        w1q, w2q, wo2q = (operand("wq%d" % i) for i in range(3))
        hq = [operand("hq%d" % k) for k in range(CHUNKS)]
        hh_rows = [sb.tile([P, PACK, W], BF16, name="hh_rows%d" % k) for k in range(CHUNKS)]
        out_sb = [sb.tile([P, G, W], F32, name="out_sb%d" % k) for k in range(CHUNKS)]
        out_rows = out.rearrange("g o n -> o g n")
        squares = [sb.tile([P, 2 * W], F32, name="squares%d" % u) for u in range(UNITS)]
        total = [sb.tile([P, W], F32, name="total%d" % u) for u in range(UNITS)]
        inv_norm = [sb.tile([P, W], F32, name="inv_norm%d" % u) for u in range(UNITS)]
        hh = [sb.tile([P, W], BF16, name="hh%d" % u) for u in range(UNITS)]

        def first_layer(k):
            for g in range(G):
                product(banks[g][k % 2][:, 0:W], g, w1q, xq[k])
                product(banks[g][k % 2][:, W:2 * W], g, w2q, xq[k])

        def square(u):
            k, g = divmod(u, G)
            nc.scalar.activation(out=squares[u][:], in_=banks[g][k % 2][:, 0:2 * W], func=FUNC.Square)

        def add(u):
            nc.vector.tensor_tensor(out=total[u][:], in0=squares[u][:, 0:W], in1=squares[u][:, W:2 * W], op=ALU.add)

        def inverse_root(u):
            g = u % G
            nc.scalar.activation(out=inv_norm[u][:], in_=total[u][:], func=FUNC.Abs_reciprocal_sqrt,
                                 bias=vec[:, ROWS * g:ROWS * g + 1])

        def scale_and_move(u):
            k, g = divmod(u, G)
            nc.vector.scalar_tensor_tensor(out=hh[u][:], in0=banks[g][k % 2][:, 0:W],
                                           scalar=vec[:, ROWS * g + 1:ROWS * g + 2], in1=inv_norm[u][:],
                                           op0=ALU.mult, op1=ALU.mult)
            nc.sync.dma_start(out=hh_rows[k][ROWS * g:ROWS * (g + 1), :, :], in_=hh[u][:])

        def second_layer(k):
            for g in range(G):
                product(banks[g][k % 2][:, 2 * W:3 * W], g, wo2q, hq[k])

        def add_residual(k, groups):
            for g in groups:
                nc.vector.tensor_tensor(out=out_sb[k][:, g, :], in0=banks[g][k % 2][:, 2 * W:3 * W],
                                        in1=res_sb[:, g, k * W:(k + 1) * W], op=ALU.add)

        def store(queue, k, g0, g1):
            queue.dma_start(out=out_rows[:, g0:g1, k * W:(k + 1) * W], in_=out_sb[k][:, g0:g1, :])

        interleave(nc.vector.tensor_copy, xq[0][0][:], x_chunk(0))
        nc.vector.transpose(vec[:], vec_rows[:])
        quantize(xq[0])
        interleave(nc.vector.tensor_copy, w1q[0][:], w_raw[0][:])
        interleave(nc.scalar.copy, w2q[0][:, 0:SCALAR_COLS, :], w_raw[1][:, :, 0:SCALAR_COLS])
        interleave(nc.vector.tensor_copy, w2q[0][:, SCALAR_COLS:M, :], w_raw[1][:, :, SCALAR_COLS:M])
        quantize(w1q)
        quantize(w2q)
        first_layer(0)
        interleave(nc.scalar.copy, wo2q[0][:], w_raw[2][:])
        interleave(nc.vector.tensor_copy, xq[1][0][:], x_chunk(1))

        def last_read_step(k):
            return G * (k + 1) - 1 + LAG

        for step in range(UNITS + LAG):
            if step < UNITS:
                square(step)
            if step >= LAG:
                inverse_root(step - LAG)
            if step < UNITS:
                add(step)
            if step >= LAG:
                scale_and_move(step - LAG)

            for k in range(1, CHUNKS):
                quantize_step = G * (k - 1)
                if step == quantize_step - 1:
                    interleave(nc.vector.tensor_copy, xq[k][0][:], x_chunk(k))
                if step == quantize_step:
                    quantize(xq[k])
                banks_free_step = last_read_step(k - 2) if k >= 2 else 0
                if step == max(quantize_step, banks_free_step):
                    first_layer(k)
            if step == WO_STEP:
                quantize(wo2q)
            if step == HH_STEP:
                interleave(nc.vector.tensor_copy, hq[0][0][:], hh_rows[0][:])
            if step == HH_STEP + 1:
                quantize(hq[0])
            if step == last_read_step(2):
                second_layer(0)

        half = G // 2
        for k in range(1, CHUNKS):
            done, first = k - 1, RESIDUALS_FIRST[k - 1]
            in_halves = done == CHUNKS - 2
            interleave(nc.scalar.copy, hq[k][0][:], hh_rows[k][:])
            add_residual(done, range(first))
            if in_halves:
                store(nc.sync, done, 0, half)
            quantize(hq[k])
            second_layer(k)
            add_residual(done, range(first, G))
            if in_halves:
                store(nc.scalar, done, half, G)
            else:
                store(nc.sync, done, 0, G)
        for queue, g0 in ((nc.sync, 0), (nc.scalar, half)):
            add_residual(CHUNKS - 1, range(g0, g0 + half))
            store(queue, CHUNKS - 1, g0, g0 + half)
